import numpy as np
import ml_dtypes


def mxq(x, axis, fmt="e4m3"):
    dtype, down = {"e4m3": (ml_dtypes.float8_e4m3fn, 7), "e5m2": (ml_dtypes.float8_e5m2, 14)}[fmt]
    v = np.moveaxis(np.asarray(x, np.float32).astype(ml_dtypes.bfloat16).astype(np.float64), axis, -1)
    blocks = v.reshape(v.shape[:-1] + (-1, 32))
    amax = np.abs(blocks).max(-1, keepdims=True)
    byte = np.maximum(np.where(amax > 0, np.frexp(amax)[1] - 1 + 127, 0) - down, 1)
    scale = np.exp2(byte - 127.0)
    codes = (blocks / scale).astype(np.float32).astype(dtype).astype(np.float64)
    return np.moveaxis((codes * scale).reshape(v.shape), -1, axis)


WIDE = False


def mx_kscale(k):
    if not WIDE:
        return np.ones(k)
    levels = np.array([10, -10, 5, -5, 0])
    if k % 512:
        return np.exp2(np.random.permutation(np.resize(levels, k // 32))).repeat(32)
    a = np.empty((k // 512, 16))
    for p in range(k // 512):
        a[p, :8] = np.random.permutation(np.resize(levels, 8))
        for g in range(8):
            far = levels[np.abs(levels - a[p, g]) >= 10]
            a[p, g + 8] = far[np.random.randint(len(far))]
    return np.exp2(a.ravel()).repeat(32)


def f64(x):
    return np.asarray(x).astype(np.float64)


def striped(idx):
    return np.tile(idx.reshape(-1, 16).T, (8, 1)).astype(np.uint16)


def unstriped(offs):
    return offs[:16].T.reshape(-1).astype(np.int64)


K, T, D, S, V, R, N = 512, 2048, 5, 1280, 256, 8, 256


def setup_inputs():
    n = np.random.standard_normal
    s = mx_kscale(K)[:, None]
    return {
        "xT": (n((K, T)) * s).astype(np.float32),
        "w": (n((D, K, N)) / np.sqrt(D * K) / s[None]).astype(np.float32),
        "b": (0.3 * n((N, 1))).astype(np.float32),
        "offs": striped(np.concatenate([R * np.arange(V) + np.random.randint(0, R, V) for _ in range(D)])),
    }


def reference(xT, w, b, offs):
    idx = unstriped(offs)
    xq = mxq(f64(xT)[:, idx], 0, "e4m3")
    wq = mxq(f64(w), 1, "e4m3")
    y = sum(wq[d].T @ xq[:, d * V:(d + 1) * V] for d in range(D))
    y = y + f64(b)
    return y

@@ -1,0 +1,140 @@
+from contextlib import ExitStack
+
+import concourse.mybir as mybir
+from concourse.masks import make_identity
+
+K, T, D, V, R, N = 512, 2048, 5, 256, 8, 256
+S = D * V
+FLOPS = 2 * K * S * N
+
+F32 = mybir.dt.float32
+BF16 = mybir.dt.bfloat16
+U32 = mybir.dt.uint32
+U16 = mybir.dt.uint16
+U8 = mybir.dt.uint8
+FP8X4 = mybir.dt.float8_e4m3fn_x4
+COPY = mybir.ActivationFunctionType.Copy
+IDENT = mybir.ActivationFunctionType.Identity
+ADD = mybir.AluOpType.add
+
+P = 128
+PACK = 4
+X_CHUNKS = [1024,512,512]
+X_CASTS = [[("v", 0, 512), ("s", 512, 256), ("s", 768, 256)], [("v", 0, 256), ("s", 256, 256)], [("v", 0, 256), ("s", 256, 256)]]
+X_QUANTS = [[(512, 256), (0, 512), (768, 256)], [(0, 256), (256, 256)], [(256, 256), (0, 256)]]
+EARLY = 192
+
+
+def interleave(nc, engine, grouped, raw, c0, n):
+    dst = grouped[:, c0 : c0 + n, :].rearrange("p (c i) t -> p c t i", i=4)
+    src = raw[:, :, c0 : c0 + n].rearrange("p t (c i) -> p c t i", i=4)
+    if engine == "v":
+        nc.vector.tensor_copy(out=dst, in_=src)
+    else:
+        nc.scalar.activation(out=dst, in_=src, func=COPY)
+
+
+def quantize(nc, codes, scales, grouped, c0, n, o0):
+    nc.vector.quantize_mx(
+        out=codes[:, o0 : o0 + n].bitcast(FP8X4),
+        scales=scales[:, o0 : o0 + n],
+        in_=grouped[:, c0 : c0 + n, :].rearrange("p c t -> p (c t)"),
+    )
+
+
+def tile_picked_deform_lin_bias_def_e_kernel(tc, xT, w, b, offs, out):
+    nc = tc.nc
+    with ExitStack() as ctx:
+        keep = ctx.enter_context(tc.tile_pool(name="keep", bufs=1))
+        psum = ctx.enter_context(tc.psum_pool(name="psum", bufs=1))
+
+        offsets = keep.tile([P, S // 16], U16, name="offsets")
+        x_codes = keep.tile([P, T], U32, name="x_codes", align_bytes=64)
+        x_scales = keep.tile([P, T], U8, name="x_scales", align_bytes=64)
+        g_codes = keep.tile([P, S], U32, name="g_codes", align_bytes=64)
+        g_scales = keep.tile([P, S], U8, name="g_scales", align_bytes=64)
+        w_codes = keep.tile([P, D * N], U32, name="w_codes", align_bytes=64)
+        w_scales = keep.tile([P, D * N], U8, name="w_scales", align_bytes=64)
+        x_raw = [keep.tile([P, PACK, n], F32, name=f"x_raw{c}", align_bytes=64) for c, n in enumerate(X_CHUNKS)]
+        x_grp = [keep.tile([P, n, PACK], BF16, name=f"x_grp{c}", align_bytes=64) for c, n in enumerate(X_CHUNKS)]
+        w_raw = [keep.tile([P, PACK, N], F32, name=f"w_raw{d}", align_bytes=64) for d in range(D)]
+        w_grp = [keep.tile([P, N, PACK], BF16, name=f"w_grp{d}", align_bytes=64) for d in range(D)]
+        ident = keep.tile([P, P], F32, name="ident")
+        b_rows = keep.tile([P, P], F32, name="b_rows")
+        bias = keep.tile([P, 2], F32, name="bias")
+        warm = keep.tile([P, 8], F32, name="warm")
+        res = [keep.tile([P, V], F32, name=f"res{h}") for h in range(2)]
+        acc = [psum.tile([P, V], F32, name=f"acc{h}") for h in range(2)]
+        b_cols = psum.tile([P, P], F32, name="b_cols")
+
+        starts = [sum(X_CHUNKS[:c]) for c in range(len(X_CHUNKS))]
+        x_view = xT.rearrange("(p j) t -> p j t", j=PACK)
+
+        nc.vector.memset(b_rows[:], 0.0)
+        nc.scalar.activation(out=warm[:], in_=b_rows[:, 64:72], func=IDENT)
+        nc.gpsimd.memset(x_scales[:], 0)
+        make_identity(nc, ident[:])
+
+        for c, n in enumerate(X_CHUNKS):
+            nc.sync.dma_start(out=x_raw[c][:], in_=x_view[:, :, starts[c] : starts[c] + n])
+            if c == 0:
+                nc.sync.dma_start(offsets[:], offs)
+            if c == 1:
+                nc.sync.dma_start(out=b_rows[0:2, :], in_=b.rearrange("(h m) o -> h (m o)", h=2))
+        for d in range(D):
+            nc.sync.dma_start(out=w_raw[d][:], in_=w[d].rearrange("(p j) n -> p j n", j=PACK))
+
+        def gather(e0, e1, window):
+            sl = offsets[:, e0 // 16 : e1 // 16]
+            nc.vector.tensor_copy(g_codes[:, e0:e1], x_codes[:, :window].indirect(sl))
+            nc.vector.tensor_copy(g_scales[:, e0:e1], x_scales[:, :window].indirect(sl))
+
+        def passes(d):
+            for h in range(2):
+                wc = slice(d * N + h * P, d * N + (h + 1) * P)
+                gc = slice(d * V, (d + 1) * V)
+                nc.tensor.matmul_mx(
+                    out=acc[h][:],
+                    lhsT=w_codes[:, wc].bitcast(FP8X4),
+                    lhsT_scale=w_scales[:, wc],
+                    rhs=g_codes[:, gc].bitcast(FP8X4),
+                    rhs_scale=g_scales[:, gc],
+                    start=(d == 0),
+                    stop=(d == D - 1),
+                )
+
+        last = len(X_CHUNKS) - 1
+        for c in range(len(X_CHUNKS)):
+            if c == last and EARLY:
+                for d in (0, 2):
+                    gather(d * V, d * V + EARLY, R * EARLY)
+            for engine, c0, n in X_CASTS[c]:
+                interleave(nc, engine, x_grp[c], x_raw[c], c0, n)
+            for c0, n in X_QUANTS[c]:
+                quantize(nc, x_codes, x_scales, x_grp[c], c0, n, starts[c] + c0)
+            if c == 0:
+                nc.tensor.transpose(b_cols[:], b_rows[:], ident[:])
+                nc.scalar.activation(out=bias[:], in_=b_cols[:, 0:2], func=COPY)
+
+        for d in range(D - 1):
+            interleave(nc, "s", w_grp[d], w_raw[d], 0, N)
+        gather(EARLY, 2 * V, T)
+        quantize(nc, w_codes, w_scales, w_grp[0], 0, N, 0)
+        quantize(nc, w_codes, w_scales, w_grp[1], 0, N, N)
+        passes(0)
+        passes(1)
+        gather(2 * V + EARLY, S, T)
+        quantize(nc, w_codes, w_scales, w_grp[2], 0, N, 2 * N)
+        quantize(nc, w_codes, w_scales, w_grp[3], 0, N, 3 * N)
+        passes(2)
+        passes(3)
+        interleave(nc, "v", w_grp[4], w_raw[4], 0, P)
+        interleave(nc, "s", w_grp[4], w_raw[4], P, P)
+        quantize(nc, w_codes, w_scales, w_grp[4], 0, P, 4 * N)
+        quantize(nc, w_codes, w_scales, w_grp[4], P, P, 4 * N + P)
+        passes(4)
+
+        nc.vector.tensor_scalar(out=res[0][:], in0=acc[0][:], scalar1=bias[:, 0:1], scalar2=None, op0=ADD)
+        nc.scalar.activation(out=res[1][:], in_=acc[1][:], func=IDENT, bias=bias[:, 1:2])
+        nc.sync.dma_start(out=out[0:P, :], in_=res[0][:])
+        nc.scalar.dma_start(out=out[P:N, :], in_=res[1][:])

@@ -19,10 +19,11 @@ ADD = mybir.AluOpType.add
 
 P = 128
 PACK = 4
-X_CHUNKS = [1024,512,512]
-X_CASTS = [[("v", 0, 512), ("s", 512, 256), ("s", 768, 256)], [("v", 0, 256), ("s", 256, 256)], [("v", 0, 256), ("s", 256, 256)]]
-X_QUANTS = [[(512, 256), (0, 512), (768, 256)], [(0, 256), (256, 256)], [(256, 256), (0, 256)]]
-EARLY = 192
+X_CHUNKS = [1024,512,256,256]
+X_CASTS = [[("v", 0, 512), ("s", 512, 256), ("s", 768, 256)], [("v", 0, 192), ("s", 256, 256), ("s", 192, 64)], [("s", 0, 256)], [("v", 0, 128), ("s", 128, 128)]]
+X_QUANTS = [[(512, 256), (0, 512), (768, 256)], [(256, 256), (0, 256)], [(0, 256)], [(0, 128), (128, 128)]]
+EARLY = 128
+EARLY_AT = 1
 
 
 def interleave(nc, engine, grouped, raw, c0, n):
@@ -62,6 +63,7 @@ def tile_picked_deform_lin_bias_def_e_kernel(tc, xT, w, b, offs, out):
         ident = keep.tile([P, P], F32, name="ident")
         b_rows = keep.tile([P, P], F32, name="b_rows")
         bias = keep.tile([P, 2], F32, name="bias")
+        warm_in = keep.tile([P, 8], F32, name="warm_in")
         warm = keep.tile([P, 8], F32, name="warm")
         res = [keep.tile([P, V], F32, name=f"res{h}") for h in range(2)]
         acc = [psum.tile([P, V], F32, name=f"acc{h}") for h in range(2)]
@@ -71,16 +73,18 @@ def tile_picked_deform_lin_bias_def_e_kernel(tc, xT, w, b, offs, out):
         x_view = xT.rearrange("(p j) t -> p j t", j=PACK)
 
         nc.vector.memset(b_rows[:], 0.0)
-        nc.scalar.activation(out=warm[:], in_=b_rows[:, 64:72], func=IDENT)
+        nc.vector.memset(warm_in[:], 0.0)
+        nc.scalar.dma_start(out=b_rows[0:2, :], in_=b.rearrange("(h m) o -> h (m o)", h=2))
+        nc.scalar.activation(out=warm[:], in_=warm_in[:], func=IDENT)
         nc.gpsimd.memset(x_scales[:], 0)
         make_identity(nc, ident[:])
+        nc.tensor.transpose(b_cols[:], b_rows[:], ident[:])
+        nc.scalar.activation(out=bias[:], in_=b_cols[:, 0:2], func=COPY)
 
         for c, n in enumerate(X_CHUNKS):
             nc.sync.dma_start(out=x_raw[c][:], in_=x_view[:, :, starts[c] : starts[c] + n])
             if c == 0:
                 nc.sync.dma_start(offsets[:], offs)
-            if c == 1:
-                nc.sync.dma_start(out=b_rows[0:2, :], in_=b.rearrange("(h m) o -> h (m o)", h=2))
         for d in range(D):
             nc.sync.dma_start(out=w_raw[d][:], in_=w[d].rearrange("(p j) n -> p j n", j=PACK))
 
@@ -90,7 +94,7 @@ def tile_picked_deform_lin_bias_def_e_kernel(tc, xT, w, b, offs, out):
             nc.vector.tensor_copy(g_scales[:, e0:e1], x_scales[:, :window].indirect(sl))
 
         def passes(d):
-            for h in range(2):
+            for h in (1, 0):
                 wc = slice(d * N + h * P, d * N + (h + 1) * P)
                 gc = slice(d * V, (d + 1) * V)
                 nc.tensor.matmul_mx(
@@ -103,38 +107,35 @@ def tile_picked_deform_lin_bias_def_e_kernel(tc, xT, w, b, offs, out):
                     stop=(d == D - 1),
                 )
 
-        last = len(X_CHUNKS) - 1
         for c in range(len(X_CHUNKS)):
-            if c == last and EARLY:
-                for d in (0, 2):
-                    gather(d * V, d * V + EARLY, R * EARLY)
             for engine, c0, n in X_CASTS[c]:
                 interleave(nc, engine, x_grp[c], x_raw[c], c0, n)
+            if c == EARLY_AT:
+                for d in (0, 2):
+                    gather(d * V, d * V + EARLY, R * EARLY)
             for c0, n in X_QUANTS[c]:
                 quantize(nc, x_codes, x_scales, x_grp[c], c0, n, starts[c] + c0)
-            if c == 0:
-                nc.tensor.transpose(b_cols[:], b_rows[:], ident[:])
-                nc.scalar.activation(out=bias[:], in_=b_cols[:, 0:2], func=COPY)
 
         for d in range(D - 1):
             interleave(nc, "s", w_grp[d], w_raw[d], 0, N)
         gather(EARLY, 2 * V, T)
         quantize(nc, w_codes, w_scales, w_grp[0], 0, N, 0)
-        quantize(nc, w_codes, w_scales, w_grp[1], 0, N, N)
         passes(0)
+        quantize(nc, w_codes, w_scales, w_grp[1], 0, N, N)
         passes(1)
-        gather(2 * V + EARLY, S, T)
+        gather(2 * V + EARLY, 4 * V, T)
         quantize(nc, w_codes, w_scales, w_grp[2], 0, N, 2 * N)
-        quantize(nc, w_codes, w_scales, w_grp[3], 0, N, 3 * N)
         passes(2)
+        gather(4 * V, S, T)
+        quantize(nc, w_codes, w_scales, w_grp[3], 0, N, 3 * N)
         passes(3)
         interleave(nc, "v", w_grp[4], w_raw[4], 0, P)
         interleave(nc, "s", w_grp[4], w_raw[4], P, P)
-        quantize(nc, w_codes, w_scales, w_grp[4], 0, P, 4 * N)
         quantize(nc, w_codes, w_scales, w_grp[4], P, P, 4 * N + P)
+        quantize(nc, w_codes, w_scales, w_grp[4], 0, P, 4 * N)
         passes(4)
 
-        nc.vector.tensor_scalar(out=res[0][:], in0=acc[0][:], scalar1=bias[:, 0:1], scalar2=None, op0=ADD)
         nc.scalar.activation(out=res[1][:], in_=acc[1][:], func=IDENT, bias=bias[:, 1:2])
-        nc.sync.dma_start(out=out[0:P, :], in_=res[0][:])
         nc.scalar.dma_start(out=out[P:N, :], in_=res[1][:])
+        nc.vector.tensor_scalar(out=res[0][:], in0=acc[0][:], scalar1=bias[:, 0:1], scalar2=None, op0=ADD)
+        nc.sync.dma_start(out=out[0:P, :], in_=res[0][:])

from contextlib import ExitStack

import concourse.mybir as mybir
from concourse.masks import make_identity

K, T, D, V, R, N = 512, 2048, 5, 256, 8, 256
S = D * V
FLOPS = 2 * K * S * N

F32 = mybir.dt.float32
BF16 = mybir.dt.bfloat16
U32 = mybir.dt.uint32
U16 = mybir.dt.uint16
U8 = mybir.dt.uint8
FP8X4 = mybir.dt.float8_e4m3fn_x4
COPY = mybir.ActivationFunctionType.Copy
IDENT = mybir.ActivationFunctionType.Identity
ADD = mybir.AluOpType.add

P = 128
PACK = 4
X_CHUNKS = [1024,512,256,256]
X_CASTS = [[("v", 0, 512), ("s", 512, 256), ("s", 768, 256)], [("v", 0, 192), ("s", 256, 256), ("s", 192, 64)], [("s", 0, 256)], [("v", 0, 128), ("s", 128, 128)]]
X_QUANTS = [[(512, 256), (0, 512), (768, 256)], [(256, 256), (0, 256)], [(0, 256)], [(0, 128), (128, 128)]]
EARLY = 128
EARLY_AT = 1


def interleave(nc, engine, grouped, raw, c0, n):
    dst = grouped[:, c0 : c0 + n, :].rearrange("p (c i) t -> p c t i", i=4)
    src = raw[:, :, c0 : c0 + n].rearrange("p t (c i) -> p c t i", i=4)
    if engine == "v":
        nc.vector.tensor_copy(out=dst, in_=src)
    else:
        nc.scalar.activation(out=dst, in_=src, func=COPY)


def quantize(nc, codes, scales, grouped, c0, n, o0):
    nc.vector.quantize_mx(
        out=codes[:, o0 : o0 + n].bitcast(FP8X4),
        scales=scales[:, o0 : o0 + n],
        in_=grouped[:, c0 : c0 + n, :].rearrange("p c t -> p (c t)"),
    )


def tile_picked_deform_lin_bias_def_e_kernel(tc, xT, w, b, offs, out):
    nc = tc.nc
    with ExitStack() as ctx:
        keep = ctx.enter_context(tc.tile_pool(name="keep", bufs=1))
        psum = ctx.enter_context(tc.psum_pool(name="psum", bufs=1))

        offsets = keep.tile([P, S // 16], U16, name="offsets")
        x_codes = keep.tile([P, T], U32, name="x_codes", align_bytes=64)
        x_scales = keep.tile([P, T], U8, name="x_scales", align_bytes=64)
        g_codes = keep.tile([P, S], U32, name="g_codes", align_bytes=64)
        g_scales = keep.tile([P, S], U8, name="g_scales", align_bytes=64)
        w_codes = keep.tile([P, D * N], U32, name="w_codes", align_bytes=64)
        w_scales = keep.tile([P, D * N], U8, name="w_scales", align_bytes=64)
        x_raw = [keep.tile([P, PACK, n], F32, name=f"x_raw{c}", align_bytes=64) for c, n in enumerate(X_CHUNKS)]
        x_grp = [keep.tile([P, n, PACK], BF16, name=f"x_grp{c}", align_bytes=64) for c, n in enumerate(X_CHUNKS)]
        w_raw = [keep.tile([P, PACK, N], F32, name=f"w_raw{d}", align_bytes=64) for d in range(D)]
        w_grp = [keep.tile([P, N, PACK], BF16, name=f"w_grp{d}", align_bytes=64) for d in range(D)]
        ident = keep.tile([P, P], F32, name="ident")
        b_rows = keep.tile([P, P], F32, name="b_rows")
        bias = keep.tile([P, 2], F32, name="bias")
        warm_in = keep.tile([P, 8], F32, name="warm_in")
        warm = keep.tile([P, 8], F32, name="warm")
        res = [keep.tile([P, V], F32, name=f"res{h}") for h in range(2)]
        acc = [psum.tile([P, V], F32, name=f"acc{h}") for h in range(2)]
        b_cols = psum.tile([P, P], F32, name="b_cols")

        starts = [sum(X_CHUNKS[:c]) for c in range(len(X_CHUNKS))]
        x_view = xT.rearrange("(p j) t -> p j t", j=PACK)

        nc.vector.memset(b_rows[:], 0.0)
        nc.vector.memset(warm_in[:], 0.0)
        nc.scalar.dma_start(out=b_rows[0:2, :], in_=b.rearrange("(h m) o -> h (m o)", h=2))
        nc.scalar.activation(out=warm[:], in_=warm_in[:], func=IDENT)
        nc.gpsimd.memset(x_scales[:], 0)
        make_identity(nc, ident[:])
        nc.tensor.transpose(b_cols[:], b_rows[:], ident[:])
        nc.scalar.activation(out=bias[:], in_=b_cols[:, 0:2], func=COPY)

        for c, n in enumerate(X_CHUNKS):
            nc.sync.dma_start(out=x_raw[c][:], in_=x_view[:, :, starts[c] : starts[c] + n])
            if c == 0:
                nc.sync.dma_start(offsets[:], offs)
        for d in range(D):
            nc.sync.dma_start(out=w_raw[d][:], in_=w[d].rearrange("(p j) n -> p j n", j=PACK))

        def gather(e0, e1, window):
            sl = offsets[:, e0 // 16 : e1 // 16]
            nc.vector.tensor_copy(g_codes[:, e0:e1], x_codes[:, :window].indirect(sl))
            nc.vector.tensor_copy(g_scales[:, e0:e1], x_scales[:, :window].indirect(sl))

        def passes(d):
            for h in (1, 0):
                wc = slice(d * N + h * P, d * N + (h + 1) * P)
                gc = slice(d * V, (d + 1) * V)
                nc.tensor.matmul_mx(
                    out=acc[h][:],
                    lhsT=w_codes[:, wc].bitcast(FP8X4),
                    lhsT_scale=w_scales[:, wc],
                    rhs=g_codes[:, gc].bitcast(FP8X4),
                    rhs_scale=g_scales[:, gc],
                    start=(d == 0),
                    stop=(d == D - 1),
                )

        for c in range(len(X_CHUNKS)):
            for engine, c0, n in X_CASTS[c]:
                interleave(nc, engine, x_grp[c], x_raw[c], c0, n)
            if c == EARLY_AT:
                for d in (0, 2):
                    gather(d * V, d * V + EARLY, R * EARLY)
            for c0, n in X_QUANTS[c]:
                quantize(nc, x_codes, x_scales, x_grp[c], c0, n, starts[c] + c0)

        for d in range(D - 1):
            interleave(nc, "s", w_grp[d], w_raw[d], 0, N)
        gather(EARLY, 2 * V, T)
        quantize(nc, w_codes, w_scales, w_grp[0], 0, N, 0)
        passes(0)
        quantize(nc, w_codes, w_scales, w_grp[1], 0, N, N)
        passes(1)
        gather(2 * V + EARLY, 4 * V, T)
        quantize(nc, w_codes, w_scales, w_grp[2], 0, N, 2 * N)
        passes(2)
        gather(4 * V, S, T)
        quantize(nc, w_codes, w_scales, w_grp[3], 0, N, 3 * N)
        passes(3)
        interleave(nc, "v", w_grp[4], w_raw[4], 0, P)
        interleave(nc, "s", w_grp[4], w_raw[4], P, P)
        quantize(nc, w_codes, w_scales, w_grp[4], P, P, 4 * N + P)
        quantize(nc, w_codes, w_scales, w_grp[4], 0, P, 4 * N)
        passes(4)

        nc.scalar.activation(out=res[1][:], in_=acc[1][:], func=IDENT, bias=bias[:, 1:2])
        nc.scalar.dma_start(out=out[P:N, :], in_=res[1][:])
        nc.vector.tensor_scalar(out=res[0][:], in0=acc[0][:], scalar1=bias[:, 0:1], scalar2=None, op0=ADD)
        nc.sync.dma_start(out=out[0:P, :], in_=res[0][:])
